import numpy as np
import ml_dtypes


def mxq(x, axis, fmt="e4m3"):
    dtype, down = {"e4m3": (ml_dtypes.float8_e4m3fn, 7), "e5m2": (ml_dtypes.float8_e5m2, 14)}[fmt]
    v = np.moveaxis(np.asarray(x, np.float32).astype(ml_dtypes.bfloat16).astype(np.float64), axis, -1)
    blocks = v.reshape(v.shape[:-1] + (-1, 32))
    amax = np.abs(blocks).max(-1, keepdims=True)
    byte = np.maximum(np.where(amax > 0, np.frexp(amax)[1] - 1 + 127, 0) - down, 1)
    scale = np.exp2(byte - 127.0)
    codes = (blocks / scale).astype(np.float32).astype(dtype).astype(np.float64)
    return np.moveaxis((codes * scale).reshape(v.shape), -1, axis)


WIDE = False


def mx_kscale(k):
    if not WIDE:
        return np.ones(k)
    levels = np.array([10, -10, 5, -5, 0])
    if k % 512:
        return np.exp2(np.random.permutation(np.resize(levels, k // 32))).repeat(32)
    a = np.empty((k // 512, 16))
    for p in range(k // 512):
        a[p, :8] = np.random.permutation(np.resize(levels, 8))
        for g in range(8):
            far = levels[np.abs(levels - a[p, g]) >= 10]
            a[p, g + 8] = far[np.random.randint(len(far))]
    return np.exp2(a.ravel()).repeat(32)


def f64(x):
    return np.asarray(x).astype(np.float64)


def striped(idx):
    return np.tile(np.asarray(idx).reshape(-1, 16).T, (8, 1)).astype(np.uint16)


def unstriped(offs):
    return offs[:16].T.reshape(-1).astype(np.int64)


E2M1 = np.array([0.0, 0.5, 1.0, 1.5, 2.0, 3.0, 4.0, 6.0, -0.0, -0.5, -1.0, -1.5, -2.0, -3.0, -4.0, -6.0])


def pack_weight(w, fmt):
    k, n = w.shape
    w = f64(np.asarray(w, np.float32).astype(ml_dtypes.bfloat16)).reshape(k // 32, 32, n)
    amax = np.abs(w).max(1)
    if fmt == "e4m3":
        byte = np.frexp(amax)[1] - 1 + 127 - 7
    else:
        mant, ex = np.frexp(amax / 6.0)
        byte = np.where(mant > 0.5, ex, ex - 1) + 127
    byte = np.clip(np.where(amax > 0, byte, 1), 1, 254)
    scaled = (w * np.exp2(127.0 - byte)[:, None, :]).reshape(k, n).astype(np.float32)
    by_word = np.ascontiguousarray(scaled.reshape(k // 512, 128, 4, n).transpose(0, 1, 3, 2))
    if fmt == "e4m3":
        words = by_word.astype(ml_dtypes.float8_e4m3fn).view(np.uint8)
    else:
        c = by_word.astype(ml_dtypes.float4_e2m1fn).view(np.uint8) & 0xF
        words = (c[..., 0::2] | (c[..., 1::2] << 4)).reshape(k // 512, 128, 2 * n)
    return np.ascontiguousarray(words), np.ascontiguousarray(byte.astype(np.uint8).reshape(k // 512, 16, n))


def unpack_weight(words, scales, fmt):
    g, _, n = scales.shape
    words = np.ascontiguousarray(words).reshape(g, 128, n, -1)
    if fmt == "e4m3":
        vals = words.view(ml_dtypes.float8_e4m3fn).astype(np.float64)
    else:
        nib = np.empty((g, 128, n, 4), np.uint8)
        nib[..., 0::2] = words & 0xF
        nib[..., 1::2] = words >> 4
        vals = E2M1[nib]
    vals = vals * np.repeat(np.exp2(scales.astype(np.float64) - 127.0), 8, axis=1)[..., None]
    return vals.transpose(0, 1, 3, 2).reshape(g * 512, n)


B, N, T, D, DV, NQ = 2, 512, 2048, 512, 256, 256


def setup_inputs():
    n = np.random.standard_normal
    seg = T // B
    idx = np.concatenate([b * seg + np.random.permutation(seg)[:N] for b in range(B)])
    s = mx_kscale(D)[:, None]
    u = np.ones(T)
    u[idx] = mx_kscale(B * N)
    r = np.random.uniform(0.5, 2.0, T)
    k = n((D, T)) / s
    v = n((DV, T)) / (u * r)
    kp = pack_weight(k, "e4m3")
    return {
        "qT": (n((B, D, NQ)) * s * (1.00 / np.sqrt(D))).astype(np.float32),
        "k_words": kp[0],
        "k_scales": kp[1],
        "vT": v.astype(np.float32),
        "vs": np.tile(u * r, (128, 1)).astype(np.float32),
        "og": n((B, NQ, DV)).astype(np.float32),
        "offs": striped(idx),
    }


def reference(qT, k_words, k_scales, vT, vs, og, offs):
    idx = unstriped(offs)
    k = unpack_weight(k_words, k_scales, "e4m3")
    v = f64(vT)
    pick = lambda x: x[:, idx].reshape(x.shape[0], B, N).transpose(1, 0, 2)
    q = f64(qT)
    score = mxq(q, 1, "e4m3").transpose(0, 2, 1) @ pick(k)
    m = score.max(-1, keepdims=True)
    p = np.exp(score - m)
    total = p.sum(-1, keepdims=True)
    w = p * pick(f64(vs))[:, :1, :]
    y = mxq(w, 2, "e4m3") @ mxq(pick(v).transpose(0, 2, 1), 1, "e4m3")
    y = y / total
    y = y / (1.0 + np.exp(-f64(og)))
    return y

@@ -1,0 +1,216 @@
+from contextlib import ExitStack
+
+import concourse.mybir as mybir
+from concourse.masks import make_identity
+
+B, N, T, D, DV, NQ = 2, 512, 2048, 512, 256, 256
+FLOPS = 2 * B * NQ * N * (D + DV)
+
+F32 = mybir.dt.float32
+BF16 = mybir.dt.bfloat16
+I32 = mybir.dt.int32
+U32 = mybir.dt.uint32
+U16 = mybir.dt.uint16
+U8 = mybir.dt.uint8
+FP8X4 = mybir.dt.float8_e4m3fn_x4
+ACT = mybir.ActivationFunctionType
+ALU = mybir.AluOpType
+AX = mybir.AxisListType
+
+P = 128
+PACK = 4
+SEG = T // B
+QT = NQ // P
+CHUNK = 512
+
+
+def tile_attend_gate_seg_kernel(tc, qT, k_words, k_scales, vT, vs, og, offs, out):
+    nc = tc.nc
+    with ExitStack() as ctx:
+        keep = ctx.enter_context(tc.tile_pool(name="keep", bufs=1))
+        psum = ctx.enter_context(tc.psum_pool(name="psum", bufs=1))
+
+        def sb(shape, dtype, name, tag=None):
+            return keep.tile(shape, dtype, name=name, tag=tag or name, align_bytes=64)
+
+        offsets = keep.tile([P, B * N // 16], U16, name="offsets")
+        nc.sync.dma_start(offsets[:], offs)
+
+        def slots(b):
+            return offsets[:, b * (N // 16):(b + 1) * (N // 16)]
+
+        key_pool = sb([P, T], I32, "key_pool")
+        kscale_pool = sb([P, T], U8, "kscale_pool")
+        vs_pool = sb([P, T], F32, "vs_pool")
+        pair_pool = sb([P, 2 * T], BF16, "pair_pool")
+        ident = sb([P, P], F32, "ident")
+        warm = sb([P, 8], F32, "warm")
+        nc.vector.memset(kscale_pool[:].bitcast(I32), 0)
+        nc.vector.memset(warm[:], 0.0)
+        nc.vector.memset(vs_pool[:], 0.0)
+        make_identity(nc, ident[:])
+
+        words_hbm = k_words[0].rearrange("p n t -> p (n t)").bitcast(I32)
+        kscales_hbm = k_scales[0].bitcast(I32)
+        v_hbm = vT.rearrange("(p h) t -> p h t", h=2)
+
+        q_raw = [sb([P, PACK, NQ], F32, "q_raw%d" % b) for b in range(B)]
+        v_raw = [sb([P, 2, CHUNK], F32, "v_raw%d" % c) for c in range(T // CHUNK)]
+        gate_raw = sb([P, B * QT, DV], F32, "gate_raw")
+
+        def load_keys(b):
+            nc.sync.dma_start(key_pool[:, b * SEG:(b + 1) * SEG], words_hbm[:, b * SEG:(b + 1) * SEG])
+
+        def load_q(b):
+            nc.sync.dma_start(q_raw[b][:], qT[b].rearrange("(p t) q -> p t q", t=PACK))
+
+        def load_v(c):
+            nc.sync.dma_start(v_raw[c][:], v_hbm[:, :, c * CHUNK:(c + 1) * CHUNK])
+
+        load_keys(0)
+        for quad in range(4):
+            nc.sync.dma_start(kscale_pool[32 * quad:32 * quad + 4, :].bitcast(I32), kscales_hbm[4 * quad:4 * quad + 4, :])
+        load_q(0)
+        nc.scalar.activation(warm[:, 0:1], warm[:, 1:2], ACT.Exp)
+        nc.scalar.dma_start(vs_pool[0:1, :], vs[0:1, :])
+        load_keys(1)
+        load_q(1)
+        load_v(0)
+        load_v(1)
+        load_v(2)
+        load_v(3)
+        nc.sync.dma_start(gate_raw[:], og.rearrange("b (h p) e -> p (b h) e", p=P))
+
+        key_codes = [sb([P, N], U32, "key_codes%d" % b) for b in range(B)]
+        key_scales = [sb([P, N], U8, "key_scales%d" % b) for b in range(B)]
+        vs_row = {}
+        vs_col = [sb([P, PACK], F32, "vs_col%d" % b) for b in range(B)]
+        v_pairs = [sb([P, N], U32, "v_pairs%d" % b) for b in range(B)]
+        q_bf = [sb([P, NQ * PACK], BF16, "q_bf%d" % b, "stage%d" % b) for b in range(B)]
+        q_codes = [sb([P, NQ], U32, "q_codes%d" % b) for b in range(B)]
+        q_scales = [sb([P, NQ], U8, "q_scales%d" % b) for b in range(B)]
+        v_bf = [sb([P, DV * PACK], BF16, "v_bf%d" % b) for b in range(B)]
+        v_codes = [sb([P, DV], U32, "v_codes%d" % b) for b in range(B)]
+        v_scales = [sb([P, DV], U8, "v_scales%d" % b) for b in range(B)]
+        tiles = range(B * QT)
+        neg_max = [sb([P, 1], F32, "neg_max%d" % j) for j in tiles]
+        total = [sb([P, QT], F32, "total%d" % b) for b in range(B)]
+        inv_total = {}
+        prob = {}
+        w_bf = [sb([P, P * PACK], BF16, "w_bf%d" % j) for j in tiles]
+        w_codes = [sb([P, P], U32, "w_codes%d" % j) for j in tiles]
+        w_scales = [sb([P, P], U8, "w_scales%d" % j) for j in tiles]
+        half_tanh = [sb([P, QT, DV], F32, "half_tanh%d" % b) for b in range(B)]
+        gate = [sb([P, QT, DV], F32, "gate%d" % b) for b in range(B)]
+        result = [sb([P, DV], F32, "result%d" % j) for j in tiles]
+        score = {}
+        prob_t = {}
+        pairs_t = {}
+
+        def window(pool_ap, b):
+            return pool_ap[:, 0:(b + 1) * SEG].indirect(slots(b))
+
+        def gather_keys(b):
+            nc.vector.tensor_copy(key_codes[b][:], window(key_pool[:].bitcast(U32), b))
+
+        def gather_key_scales(b):
+            nc.vector.tensor_copy(key_scales[b][:], window(kscale_pool[:], b))
+
+        def gather_vs(b):
+            vs_row[b] = sb([P, N], F32, "vs_row%d" % b, "stage%d" % b)
+            nc.vector.tensor_copy(vs_row[b][:], window(vs_pool[:], b))
+            nc.gpsimd.dma_start(vs_col[b][:], vs_row[b][0:1, :])
+
+        def weave_q(b):
+            nc.scalar.copy(q_bf[b][:].rearrange("p (c i t) -> p c t i", i=4, t=PACK),
+                           q_raw[b][:].rearrange("p t (c i) -> p c t i", i=4))
+
+        def quantise(codes, scales, src):
+            nc.vector.quantize_mx(out=codes[:].bitcast(FP8X4), scales=scales[:], in_=src[:])
+
+        def cast_v(c):
+            nc.scalar.copy(pair_pool[:, 2 * c * CHUNK:2 * (c + 1) * CHUNK].rearrange("p (n h) -> p n h", h=2),
+                           v_raw[c][:].rearrange("p h n -> p n h"))
+
+        def gather_v(b):
+            nc.vector.tensor_copy(v_pairs[b][:], window(pair_pool[:].bitcast(U32), b))
+            turned = psum.tile([P, PACK, P], F32, name="v_t", tag="bank%d" % (2 * b))
+            for t in range(PACK):
+                nc.tensor.transpose(turned[:, t, :], v_pairs[b][:].bitcast(F32)[:, t::PACK], ident[:])
+            pairs_t[b] = turned
+
+        def weave_v(b):
+            nc.scalar.copy(v_bf[b][:].rearrange("p (e t) -> p e t", t=PACK),
+                           pairs_t[b][:].bitcast(BF16).rearrange("p t e -> p e t"))
+
+        def scores(j):
+            b, h = divmod(j, QT)
+            cols = slice(h * P, (h + 1) * P)
+            bank = psum.tile([P, N], F32, name="score", tag="bank%d" % j)
+            nc.tensor.matmul_mx(out=bank[:], lhsT=q_codes[b][:, cols].bitcast(FP8X4), lhsT_scale=q_scales[b][:, cols],
+                                rhs=key_codes[b][:].bitcast(FP8X4), rhs_scale=key_scales[b][:], start=True, stop=True)
+            score[j] = bank
+
+        def row_max(j):
+            nc.vector.tensor_reduce(neg_max[j][:], score[j][:], AX.X, ALU.max, negate=True)
+
+        def exponent(j):
+            b, h = divmod(j, QT)
+            prob[j] = sb([P, N], F32, "prob%d" % j, "v_raw%d" % (2 * b + 1 - h))
+            nc.scalar.activation(prob[j][:].rearrange("p (t s) -> p t s", t=PACK),
+                                 score[j][:].rearrange("p (s t) -> p t s", t=PACK),
+                                 ACT.Exp, bias=neg_max[j][:], accum_out=total[b][:, h:h + 1])
+            bank = psum.tile([P, PACK, P], F32, name="prob_t", tag="bank%d" % (4 + h))
+            for t in range(PACK):
+                nc.tensor.transpose(bank[:, t, :], prob[j][:, t * P:(t + 1) * P], ident[:])
+            prob_t[j] = bank
+
+        def weights(j):
+            b = j // QT
+            nc.vector.tensor_tensor(w_bf[j][:].rearrange("p (q t) -> p q t", t=PACK),
+                                    prob_t[j][:].rearrange("p t q -> p q t"),
+                                    vs_col[b][:].unsqueeze(1).to_broadcast([P, P, PACK]), ALU.mult)
+
+        def invert(b):
+            inv_total[b] = sb([P, QT], F32, "inv_total%d" % b, "vs_col%d" % b)
+            nc.vector.reciprocal(inv_total[b][:], total[b][:])
+
+        def gates(b):
+            nc.scalar.activation(half_tanh[b][:], gate_raw[:, b * QT:(b + 1) * QT, :], ACT.Tanh, scale=0.5)
+            nc.gpsimd.tensor_scalar(gate[b][:], half_tanh[b][:], 0.5, 0.5, ALU.mult, ALU.add)
+
+        def finish(j):
+            b, h = divmod(j, QT)
+            bank = psum.tile([P, DV], F32, name="y", tag="bank%d" % (2 * b + 1 if h == 0 else 6 + b))
+            nc.tensor.matmul_mx(out=bank[:], lhsT=w_codes[j][:].bitcast(FP8X4), lhsT_scale=w_scales[j][:],
+                                rhs=v_codes[b][:].bitcast(FP8X4), rhs_scale=v_scales[b][:], start=True, stop=True)
+            nc.vector.scalar_tensor_tensor(result[j][:], bank[:], inv_total[b][:, h:h + 1], gate[b][:, h, :],
+                                           ALU.mult, ALU.mult)
+            nc.sync.dma_start(out[b, h * P:(h + 1) * P, :], result[j][:])
+
+        for b in range(B):
+            gather_keys(b)
+            gather_key_scales(b)
+            weave_q(b)
+            quantise(q_codes[b], q_scales[b], q_bf[b])
+            gather_vs(b)
+            for j in range(b * QT, (b + 1) * QT):
+                scores(j)
+                row_max(j)
+        for b in range(B):
+            cast_v(2 * b)
+            cast_v(2 * b + 1)
+            for j in range(b * QT, (b + 1) * QT):
+                exponent(j)
+            gather_v(b)
+        for b in range(B):
+            weave_v(b)
+            for j in range(b * QT, (b + 1) * QT):
+                weights(j)
+            gates(b)
+            invert(b)
+            for j in range(b * QT, (b + 1) * QT):
+                quantise(w_codes[j], w_scales[j], w_bf[j])
+            quantise(v_codes[b], v_scales[b], v_bf[b])
+            for j in range(b * QT, (b + 1) * QT):
+                finish(j)

@@ -46,8 +46,8 @@ def tile_attend_gate_seg_kernel(tc, qT, k_words, k_scales, vT, vs, og, offs, out
         ident = sb([P, P], F32, "ident")
         warm = sb([P, 8], F32, "warm")
         nc.vector.memset(kscale_pool[:].bitcast(I32), 0)
-        nc.vector.memset(warm[:], 0.0)
-        nc.vector.memset(vs_pool[:], 0.0)
+        nc.vector.memset(vs_pool[:, 0:SEG], 0.0)
+        nc.gpsimd.memset(vs_pool[:, SEG:T], 0.0)
         make_identity(nc, ident[:])
 
         words_hbm = k_words[0].rearrange("p n t -> p (n t)").bitcast(I32)
@@ -71,38 +71,38 @@ def tile_attend_gate_seg_kernel(tc, qT, k_words, k_scales, vT, vs, og, offs, out
         for quad in range(4):
             nc.sync.dma_start(kscale_pool[32 * quad:32 * quad + 4, :].bitcast(I32), kscales_hbm[4 * quad:4 * quad + 4, :])
         load_q(0)
-        nc.scalar.activation(warm[:, 0:1], warm[:, 1:2], ACT.Exp)
         nc.scalar.dma_start(vs_pool[0:1, :], vs[0:1, :])
-        load_keys(1)
-        load_q(1)
+        nc.scalar.activation(warm[32:64, 0:1], vs_pool[32:64, 0:1], ACT.Exp)
         load_v(0)
         load_v(1)
+        load_keys(1)
+        load_q(1)
         load_v(2)
         load_v(3)
         nc.sync.dma_start(gate_raw[:], og.rearrange("b (h p) e -> p (b h) e", p=P))
 
         key_codes = [sb([P, N], U32, "key_codes%d" % b) for b in range(B)]
-        key_scales = [sb([P, N], U8, "key_scales%d" % b) for b in range(B)]
+        key_scales = sb([P, B * N], U8, "key_scales")
         vs_row = {}
         vs_col = [sb([P, PACK], F32, "vs_col%d" % b) for b in range(B)]
-        v_pairs = [sb([P, N], U32, "v_pairs%d" % b) for b in range(B)]
-        q_bf = [sb([P, NQ * PACK], BF16, "q_bf%d" % b, "stage%d" % b) for b in range(B)]
+        v_pairs = {}
+        q_bf = [sb([P, NQ * PACK], BF16, "q_bf%d" % b) for b in range(B)]
         q_codes = [sb([P, NQ], U32, "q_codes%d" % b) for b in range(B)]
         q_scales = [sb([P, NQ], U8, "q_scales%d" % b) for b in range(B)]
-        v_bf = [sb([P, DV * PACK], BF16, "v_bf%d" % b) for b in range(B)]
+        v_bf = {}
         v_codes = [sb([P, DV], U32, "v_codes%d" % b) for b in range(B)]
         v_scales = [sb([P, DV], U8, "v_scales%d" % b) for b in range(B)]
         tiles = range(B * QT)
         neg_max = [sb([P, 1], F32, "neg_max%d" % j) for j in tiles]
-        total = [sb([P, QT], F32, "total%d" % b) for b in range(B)]
-        inv_total = {}
+        total = sb([P, B * QT], F32, "total")
+        inv_total = sb([P, B * QT], F32, "inv_total")
         prob = {}
-        w_bf = [sb([P, P * PACK], BF16, "w_bf%d" % j) for j in tiles]
-        w_codes = [sb([P, P], U32, "w_codes%d" % j) for j in tiles]
-        w_scales = [sb([P, P], U8, "w_scales%d" % j) for j in tiles]
+        w_bf = {}
+        w_codes = [sb([P, NQ], U32, "w_codes%d" % b) for b in range(B)]
+        w_scales = [sb([P, NQ], U8, "w_scales%d" % b) for b in range(B)]
         half_tanh = [sb([P, QT, DV], F32, "half_tanh%d" % b) for b in range(B)]
         gate = [sb([P, QT, DV], F32, "gate%d" % b) for b in range(B)]
-        result = [sb([P, DV], F32, "result%d" % j) for j in tiles]
+        result = {}
         score = {}
         prob_t = {}
         pairs_t = {}
@@ -113,13 +113,13 @@ def tile_attend_gate_seg_kernel(tc, qT, k_words, k_scales, vT, vs, og, offs, out
         def gather_keys(b):
             nc.vector.tensor_copy(key_codes[b][:], window(key_pool[:].bitcast(U32), b))
 
-        def gather_key_scales(b):
-            nc.vector.tensor_copy(key_scales[b][:], window(kscale_pool[:], b))
+        def gather_key_scales():
+            nc.vector.tensor_copy(key_scales[:], kscale_pool[:].indirect(offsets[:]))
 
         def gather_vs(b):
-            vs_row[b] = sb([P, N], F32, "vs_row%d" % b, "stage%d" % b)
+            vs_row[b] = sb([P, N], F32, "vs_row%d" % b, "q_raw0" if b == 0 else "v_raw1")
             nc.vector.tensor_copy(vs_row[b][:], window(vs_pool[:], b))
-            nc.gpsimd.dma_start(vs_col[b][:], vs_row[b][0:1, :])
+            nc.sync.dma_start(vs_col[b][:], vs_row[b][0:1, :])
 
         def weave_q(b):
             nc.scalar.copy(q_bf[b][:].rearrange("p (c i t) -> p c t i", i=4, t=PACK),
@@ -133,13 +133,15 @@ def tile_attend_gate_seg_kernel(tc, qT, k_words, k_scales, vT, vs, og, offs, out
                            v_raw[c][:].rearrange("p h n -> p n h"))
 
         def gather_v(b):
+            v_pairs[b] = sb([P, N], U32, "v_pairs%d" % b, "q_raw1" if b == 0 else None)
             nc.vector.tensor_copy(v_pairs[b][:], window(pair_pool[:].bitcast(U32), b))
-            turned = psum.tile([P, PACK, P], F32, name="v_t", tag="bank%d" % (2 * b))
+            turned = psum.tile([P, PACK, P], F32, name="v_t", tag="bank%d" % (2 * b + 1))
             for t in range(PACK):
                 nc.tensor.transpose(turned[:, t, :], v_pairs[b][:].bitcast(F32)[:, t::PACK], ident[:])
             pairs_t[b] = turned
 
         def weave_v(b):
+            v_bf[b] = sb([P, DV * PACK], BF16, "v_bf%d" % b, "v_raw%d" % (3 - b))
             nc.scalar.copy(v_bf[b][:].rearrange("p (e t) -> p e t", t=PACK),
                            pairs_t[b][:].bitcast(BF16).rearrange("p t e -> p e t"))
 
@@ -148,7 +150,7 @@ def tile_attend_gate_seg_kernel(tc, qT, k_words, k_scales, vT, vs, og, offs, out
             cols = slice(h * P, (h + 1) * P)
             bank = psum.tile([P, N], F32, name="score", tag="bank%d" % j)
             nc.tensor.matmul_mx(out=bank[:], lhsT=q_codes[b][:, cols].bitcast(FP8X4), lhsT_scale=q_scales[b][:, cols],
-                                rhs=key_codes[b][:].bitcast(FP8X4), rhs_scale=key_scales[b][:], start=True, stop=True)
+                                rhs=key_codes[b][:].bitcast(FP8X4), rhs_scale=key_scales[:, b * N:(b + 1) * N], start=True, stop=True)
             score[j] = bank
 
         def row_max(j):
@@ -156,61 +158,64 @@ def tile_attend_gate_seg_kernel(tc, qT, k_words, k_scales, vT, vs, og, offs, out
 
         def exponent(j):
             b, h = divmod(j, QT)
-            prob[j] = sb([P, N], F32, "prob%d" % j, "v_raw%d" % (2 * b + 1 - h))
+            prob[j] = sb([P, N], F32, "prob%d" % j)
             nc.scalar.activation(prob[j][:].rearrange("p (t s) -> p t s", t=PACK),
                                  score[j][:].rearrange("p (s t) -> p t s", t=PACK),
-                                 ACT.Exp, bias=neg_max[j][:], accum_out=total[b][:, h:h + 1])
-            bank = psum.tile([P, PACK, P], F32, name="prob_t", tag="bank%d" % (4 + h))
+                                 ACT.Exp, bias=neg_max[j][:], accum_out=total[:, j:j + 1])
+            bank = psum.tile([P, PACK, P], F32, name="prob_t", tag="bank%d" % (4 + j))
             for t in range(PACK):
                 nc.tensor.transpose(bank[:, t, :], prob[j][:, t * P:(t + 1) * P], ident[:])
             prob_t[j] = bank
 
         def weights(j):
-            b = j // QT
-            nc.vector.tensor_tensor(w_bf[j][:].rearrange("p (q t) -> p q t", t=PACK),
+            b, h = divmod(j, QT)
+            if h == 0:
+                w_bf[b] = sb([P, NQ * PACK], BF16, "w_bf%d" % b)
+            nc.vector.tensor_tensor(w_bf[b][:, h * N:(h + 1) * N].rearrange("p (q t) -> p q t", t=PACK),
                                     prob_t[j][:].rearrange("p t q -> p q t"),
                                     vs_col[b][:].unsqueeze(1).to_broadcast([P, P, PACK]), ALU.mult)
 
-        def invert(b):
-            inv_total[b] = sb([P, QT], F32, "inv_total%d" % b, "vs_col%d" % b)
-            nc.vector.reciprocal(inv_total[b][:], total[b][:])
-
         def gates(b):
             nc.scalar.activation(half_tanh[b][:], gate_raw[:, b * QT:(b + 1) * QT, :], ACT.Tanh, scale=0.5)
-            nc.gpsimd.tensor_scalar(gate[b][:], half_tanh[b][:], 0.5, 0.5, ALU.mult, ALU.add)
+            nc.scalar.activation(gate[b][:], half_tanh[b][:], ACT.Copy, bias=0.5, scale=0.5)
 
         def finish(j):
             b, h = divmod(j, QT)
-            bank = psum.tile([P, DV], F32, name="y", tag="bank%d" % (2 * b + 1 if h == 0 else 6 + b))
-            nc.tensor.matmul_mx(out=bank[:], lhsT=w_codes[j][:].bitcast(FP8X4), lhsT_scale=w_scales[j][:],
+            if h == 0:
+                both = sb([P, QT, DV], F32, "result%d" % b, "v_raw%d" % (2 + b))
+                for i in range(QT):
+                    result[j + i] = both[:, i, :]
+            bank = psum.tile([P, DV], F32, name="y", tag="bank%d" % (4 + j))
+            nc.tensor.matmul_mx(out=bank[:], lhsT=w_codes[b][:, h * P:(h + 1) * P].bitcast(FP8X4), lhsT_scale=w_scales[b][:, h * P:(h + 1) * P],
                                 rhs=v_codes[b][:].bitcast(FP8X4), rhs_scale=v_scales[b][:], start=True, stop=True)
-            nc.vector.scalar_tensor_tensor(result[j][:], bank[:], inv_total[b][:, h:h + 1], gate[b][:, h, :],
+            nc.vector.scalar_tensor_tensor(result[j][:], bank[:], inv_total[:, j:j + 1], gate[b][:, h, :],
                                            ALU.mult, ALU.mult)
             nc.sync.dma_start(out[b, h * P:(h + 1) * P, :], result[j][:])
 
+        gather_keys(0)
+        gather_key_scales()
         for b in range(B):
-            gather_keys(b)
-            gather_key_scales(b)
+            if b > 0:
+                gather_keys(b)
             weave_q(b)
             quantise(q_codes[b], q_scales[b], q_bf[b])
             gather_vs(b)
-            for j in range(b * QT, (b + 1) * QT):
-                scores(j)
-                row_max(j)
-        for b in range(B):
             cast_v(2 * b)
             cast_v(2 * b + 1)
             for j in range(b * QT, (b + 1) * QT):
+                scores(j)
+                row_max(j)
                 exponent(j)
+        for b in range(B):
             gather_v(b)
         for b in range(B):
             weave_v(b)
             for j in range(b * QT, (b + 1) * QT):
                 weights(j)
+        nc.vector.reciprocal(inv_total[:], total[:])
+        for b in range(B):
             gates(b)
-            invert(b)
-            for j in range(b * QT, (b + 1) * QT):
-                quantise(w_codes[j], w_scales[j], w_bf[j])
+            quantise(w_codes[b], w_scales[b], w_bf[b])
             quantise(v_codes[b], v_scales[b], v_bf[b])
-            for j in range(b * QT, (b + 1) * QT):
-                finish(j)
+        for j in range(B * QT):
+            finish(j)

@@ -71,7 +71,7 @@ def tile_attend_gate_seg_kernel(tc, qT, k_words, k_scales, vT, vs, og, offs, out
         for quad in range(4):
             nc.sync.dma_start(kscale_pool[32 * quad:32 * quad + 4, :].bitcast(I32), kscales_hbm[4 * quad:4 * quad + 4, :])
         load_q(0)
-        nc.scalar.dma_start(vs_pool[0:1, :], vs[0:1, :])
+        nc.scalar.dma_start(vs_pool[16:17, :], vs[0:1, :])
         nc.scalar.activation(warm[32:64, 0:1], vs_pool[32:64, 0:1], ACT.Exp)
         load_v(0)
         load_v(1)
@@ -119,7 +119,7 @@ def tile_attend_gate_seg_kernel(tc, qT, k_words, k_scales, vT, vs, og, offs, out
         def gather_vs(b):
             vs_row[b] = sb([P, N], F32, "vs_row%d" % b, "q_raw0" if b == 0 else "v_raw1")
             nc.vector.tensor_copy(vs_row[b][:], window(vs_pool[:], b))
-            nc.sync.dma_start(vs_col[b][:], vs_row[b][0:1, :])
+            nc.sync.dma_start(vs_col[b][:], vs_row[b][16:17, :])
 
         def weave_q(b):
             nc.scalar.copy(q_bf[b][:].rearrange("p (c i t) -> p c t i", i=4, t=PACK),

from contextlib import ExitStack

import concourse.mybir as mybir
from concourse.masks import make_identity

B, N, T, D, DV, NQ = 2, 512, 2048, 512, 256, 256
FLOPS = 2 * B * NQ * N * (D + DV)

F32 = mybir.dt.float32
BF16 = mybir.dt.bfloat16
I32 = mybir.dt.int32
U32 = mybir.dt.uint32
U16 = mybir.dt.uint16
U8 = mybir.dt.uint8
FP8X4 = mybir.dt.float8_e4m3fn_x4
ACT = mybir.ActivationFunctionType
ALU = mybir.AluOpType
AX = mybir.AxisListType

P = 128
PACK = 4
SEG = T // B
QT = NQ // P
CHUNK = 512


def tile_attend_gate_seg_kernel(tc, qT, k_words, k_scales, vT, vs, og, offs, out):
    nc = tc.nc
    with ExitStack() as ctx:
        keep = ctx.enter_context(tc.tile_pool(name="keep", bufs=1))
        psum = ctx.enter_context(tc.psum_pool(name="psum", bufs=1))

        def sb(shape, dtype, name, tag=None):
            return keep.tile(shape, dtype, name=name, tag=tag or name, align_bytes=64)

        offsets = keep.tile([P, B * N // 16], U16, name="offsets")
        nc.sync.dma_start(offsets[:], offs)

        def slots(b):
            return offsets[:, b * (N // 16):(b + 1) * (N // 16)]

        key_pool = sb([P, T], I32, "key_pool")
        kscale_pool = sb([P, T], U8, "kscale_pool")
        vs_pool = sb([P, T], F32, "vs_pool")
        pair_pool = sb([P, 2 * T], BF16, "pair_pool")
        ident = sb([P, P], F32, "ident")
        warm = sb([P, 8], F32, "warm")
        nc.vector.memset(kscale_pool[:].bitcast(I32), 0)
        nc.vector.memset(vs_pool[:, 0:SEG], 0.0)
        nc.gpsimd.memset(vs_pool[:, SEG:T], 0.0)
        make_identity(nc, ident[:])

        words_hbm = k_words[0].rearrange("p n t -> p (n t)").bitcast(I32)
        kscales_hbm = k_scales[0].bitcast(I32)
        v_hbm = vT.rearrange("(p h) t -> p h t", h=2)

        q_raw = [sb([P, PACK, NQ], F32, "q_raw%d" % b) for b in range(B)]
        v_raw = [sb([P, 2, CHUNK], F32, "v_raw%d" % c) for c in range(T // CHUNK)]
        gate_raw = sb([P, B * QT, DV], F32, "gate_raw")

        def load_keys(b):
            nc.sync.dma_start(key_pool[:, b * SEG:(b + 1) * SEG], words_hbm[:, b * SEG:(b + 1) * SEG])

        def load_q(b):
            nc.sync.dma_start(q_raw[b][:], qT[b].rearrange("(p t) q -> p t q", t=PACK))

        def load_v(c):
            nc.sync.dma_start(v_raw[c][:], v_hbm[:, :, c * CHUNK:(c + 1) * CHUNK])

        load_keys(0)
        for quad in range(4):
            nc.sync.dma_start(kscale_pool[32 * quad:32 * quad + 4, :].bitcast(I32), kscales_hbm[4 * quad:4 * quad + 4, :])
        load_q(0)
        nc.scalar.dma_start(vs_pool[16:17, :], vs[0:1, :])
        nc.scalar.activation(warm[32:64, 0:1], vs_pool[32:64, 0:1], ACT.Exp)
        load_v(0)
        load_v(1)
        load_keys(1)
        load_q(1)
        load_v(2)
        load_v(3)
        nc.sync.dma_start(gate_raw[:], og.rearrange("b (h p) e -> p (b h) e", p=P))

        key_codes = [sb([P, N], U32, "key_codes%d" % b) for b in range(B)]
        key_scales = sb([P, B * N], U8, "key_scales")
        vs_row = {}
        vs_col = [sb([P, PACK], F32, "vs_col%d" % b) for b in range(B)]
        v_pairs = {}
        q_bf = [sb([P, NQ * PACK], BF16, "q_bf%d" % b) for b in range(B)]
        q_codes = [sb([P, NQ], U32, "q_codes%d" % b) for b in range(B)]
        q_scales = [sb([P, NQ], U8, "q_scales%d" % b) for b in range(B)]
        v_bf = {}
        v_codes = [sb([P, DV], U32, "v_codes%d" % b) for b in range(B)]
        v_scales = [sb([P, DV], U8, "v_scales%d" % b) for b in range(B)]
        tiles = range(B * QT)
        neg_max = [sb([P, 1], F32, "neg_max%d" % j) for j in tiles]
        total = sb([P, B * QT], F32, "total")
        inv_total = sb([P, B * QT], F32, "inv_total")
        prob = {}
        w_bf = {}
        w_codes = [sb([P, NQ], U32, "w_codes%d" % b) for b in range(B)]
        w_scales = [sb([P, NQ], U8, "w_scales%d" % b) for b in range(B)]
        half_tanh = [sb([P, QT, DV], F32, "half_tanh%d" % b) for b in range(B)]
        gate = [sb([P, QT, DV], F32, "gate%d" % b) for b in range(B)]
        result = {}
        score = {}
        prob_t = {}
        pairs_t = {}

        def window(pool_ap, b):
            return pool_ap[:, 0:(b + 1) * SEG].indirect(slots(b))

        def gather_keys(b):
            nc.vector.tensor_copy(key_codes[b][:], window(key_pool[:].bitcast(U32), b))

        def gather_key_scales():
            nc.vector.tensor_copy(key_scales[:], kscale_pool[:].indirect(offsets[:]))

        def gather_vs(b):
            vs_row[b] = sb([P, N], F32, "vs_row%d" % b, "q_raw0" if b == 0 else "v_raw1")
            nc.vector.tensor_copy(vs_row[b][:], window(vs_pool[:], b))
            nc.sync.dma_start(vs_col[b][:], vs_row[b][16:17, :])

        def weave_q(b):
            nc.scalar.copy(q_bf[b][:].rearrange("p (c i t) -> p c t i", i=4, t=PACK),
                           q_raw[b][:].rearrange("p t (c i) -> p c t i", i=4))

        def quantise(codes, scales, src):
            nc.vector.quantize_mx(out=codes[:].bitcast(FP8X4), scales=scales[:], in_=src[:])

        def cast_v(c):
            nc.scalar.copy(pair_pool[:, 2 * c * CHUNK:2 * (c + 1) * CHUNK].rearrange("p (n h) -> p n h", h=2),
                           v_raw[c][:].rearrange("p h n -> p n h"))

        def gather_v(b):
            v_pairs[b] = sb([P, N], U32, "v_pairs%d" % b, "q_raw1" if b == 0 else None)
            nc.vector.tensor_copy(v_pairs[b][:], window(pair_pool[:].bitcast(U32), b))
            turned = psum.tile([P, PACK, P], F32, name="v_t", tag="bank%d" % (2 * b + 1))
            for t in range(PACK):
                nc.tensor.transpose(turned[:, t, :], v_pairs[b][:].bitcast(F32)[:, t::PACK], ident[:])
            pairs_t[b] = turned

        def weave_v(b):
            v_bf[b] = sb([P, DV * PACK], BF16, "v_bf%d" % b, "v_raw%d" % (3 - b))
            nc.scalar.copy(v_bf[b][:].rearrange("p (e t) -> p e t", t=PACK),
                           pairs_t[b][:].bitcast(BF16).rearrange("p t e -> p e t"))

        def scores(j):
            b, h = divmod(j, QT)
            cols = slice(h * P, (h + 1) * P)
            bank = psum.tile([P, N], F32, name="score", tag="bank%d" % j)
            nc.tensor.matmul_mx(out=bank[:], lhsT=q_codes[b][:, cols].bitcast(FP8X4), lhsT_scale=q_scales[b][:, cols],
                                rhs=key_codes[b][:].bitcast(FP8X4), rhs_scale=key_scales[:, b * N:(b + 1) * N], start=True, stop=True)
            score[j] = bank

        def row_max(j):
            nc.vector.tensor_reduce(neg_max[j][:], score[j][:], AX.X, ALU.max, negate=True)

        def exponent(j):
            b, h = divmod(j, QT)
            prob[j] = sb([P, N], F32, "prob%d" % j)
            nc.scalar.activation(prob[j][:].rearrange("p (t s) -> p t s", t=PACK),
                                 score[j][:].rearrange("p (s t) -> p t s", t=PACK),
                                 ACT.Exp, bias=neg_max[j][:], accum_out=total[:, j:j + 1])
            bank = psum.tile([P, PACK, P], F32, name="prob_t", tag="bank%d" % (4 + j))
            for t in range(PACK):
                nc.tensor.transpose(bank[:, t, :], prob[j][:, t * P:(t + 1) * P], ident[:])
            prob_t[j] = bank

        def weights(j):
            b, h = divmod(j, QT)
            if h == 0:
                w_bf[b] = sb([P, NQ * PACK], BF16, "w_bf%d" % b)
            nc.vector.tensor_tensor(w_bf[b][:, h * N:(h + 1) * N].rearrange("p (q t) -> p q t", t=PACK),
                                    prob_t[j][:].rearrange("p t q -> p q t"),
                                    vs_col[b][:].unsqueeze(1).to_broadcast([P, P, PACK]), ALU.mult)

        def gates(b):
            nc.scalar.activation(half_tanh[b][:], gate_raw[:, b * QT:(b + 1) * QT, :], ACT.Tanh, scale=0.5)
            nc.scalar.activation(gate[b][:], half_tanh[b][:], ACT.Copy, bias=0.5, scale=0.5)

        def finish(j):
            b, h = divmod(j, QT)
            if h == 0:
                both = sb([P, QT, DV], F32, "result%d" % b, "v_raw%d" % (2 + b))
                for i in range(QT):
                    result[j + i] = both[:, i, :]
            bank = psum.tile([P, DV], F32, name="y", tag="bank%d" % (4 + j))
            nc.tensor.matmul_mx(out=bank[:], lhsT=w_codes[b][:, h * P:(h + 1) * P].bitcast(FP8X4), lhsT_scale=w_scales[b][:, h * P:(h + 1) * P],
                                rhs=v_codes[b][:].bitcast(FP8X4), rhs_scale=v_scales[b][:], start=True, stop=True)
            nc.vector.scalar_tensor_tensor(result[j][:], bank[:], inv_total[:, j:j + 1], gate[b][:, h, :],
                                           ALU.mult, ALU.mult)
            nc.sync.dma_start(out[b, h * P:(h + 1) * P, :], result[j][:])

        gather_keys(0)
        gather_key_scales()
        for b in range(B):
            if b > 0:
                gather_keys(b)
            weave_q(b)
            quantise(q_codes[b], q_scales[b], q_bf[b])
            gather_vs(b)
            cast_v(2 * b)
            cast_v(2 * b + 1)
            for j in range(b * QT, (b + 1) * QT):
                scores(j)
                row_max(j)
                exponent(j)
        for b in range(B):
            gather_v(b)
        for b in range(B):
            weave_v(b)
            for j in range(b * QT, (b + 1) * QT):
                weights(j)
        nc.vector.reciprocal(inv_total[:], total[:])
        for b in range(B):
            gates(b)
            quantise(w_codes[b], w_scales[b], w_bf[b])
            quantise(v_codes[b], v_scales[b], v_bf[b])
        for j in range(B * QT):
            finish(j)
